import numpy as np
import ml_dtypes


def mxq(x, axis, fmt="e4m3"):
    dtype, down = {"e4m3": (ml_dtypes.float8_e4m3fn, 7), "e5m2": (ml_dtypes.float8_e5m2, 14)}[fmt]
    v = np.moveaxis(np.asarray(x, np.float32).astype(ml_dtypes.bfloat16).astype(np.float64), axis, -1)
    blocks = v.reshape(v.shape[:-1] + (-1, 32))
    amax = np.abs(blocks).max(-1, keepdims=True)
    byte = np.maximum(np.where(amax > 0, np.frexp(amax)[1] - 1 + 127, 0) - down, 1)
    scale = np.exp2(byte - 127.0)
    codes = (blocks / scale).astype(np.float32).astype(dtype).astype(np.float64)
    return np.moveaxis((codes * scale).reshape(v.shape), -1, axis)


WIDE = False


def mx_kscale(k):
    if not WIDE:
        return np.ones(k)
    levels = np.array([30, -30])
    if k % 512:
        return np.exp2(np.random.permutation(np.resize(levels, k // 32))).repeat(32)
    a = np.empty((k // 512, 16))
    for p in range(k // 512):
        a[p, :8] = np.random.permutation(np.resize(levels, 8))
        for g in range(8):
            far = levels[np.abs(levels - a[p, g]) >= 10]
            a[p, g + 8] = far[np.random.randint(len(far))]
    return np.exp2(a.ravel()).repeat(32)


def f64(x):
    return np.asarray(x).astype(np.float64)


def striped(idx):
    return np.tile(np.asarray(idx).reshape(-1, 16).T, (8, 1)).astype(np.uint16)


def unstriped(offs):
    return offs[:16].T.reshape(-1).astype(np.int64)


E2M1 = np.array([0.0, 0.5, 1.0, 1.5, 2.0, 3.0, 4.0, 6.0, -0.0, -0.5, -1.0, -1.5, -2.0, -3.0, -4.0, -6.0])


def pack_weight(w, fmt):
    k, n = w.shape
    w = f64(np.asarray(w, np.float32).astype(ml_dtypes.bfloat16)).reshape(k // 32, 32, n)
    amax = np.abs(w).max(1)
    if fmt == "e4m3":
        byte = np.frexp(amax)[1] - 1 + 127 - 7
    else:
        mant, ex = np.frexp(amax / 6.0)
        byte = np.where(mant > 0.5, ex, ex - 1) + 127
    byte = np.clip(np.where(amax > 0, byte, 1), 1, 254)
    scaled = (w * np.exp2(127.0 - byte)[:, None, :]).reshape(k, n).astype(np.float32)
    by_word = np.ascontiguousarray(scaled.reshape(k // 512, 128, 4, n).transpose(0, 1, 3, 2))
    if fmt == "e4m3":
        words = by_word.astype(ml_dtypes.float8_e4m3fn).view(np.uint8)
    else:
        c = by_word.astype(ml_dtypes.float4_e2m1fn).view(np.uint8) & 0xF
        words = (c[..., 0::2] | (c[..., 1::2] << 4)).reshape(k // 512, 128, 2 * n)
    return np.ascontiguousarray(words), np.ascontiguousarray(byte.astype(np.uint8).reshape(k // 512, 16, n))


def unpack_weight(words, scales, fmt):
    g, _, n = scales.shape
    words = np.ascontiguousarray(words).reshape(g, 128, n, -1)
    if fmt == "e4m3":
        vals = words.view(ml_dtypes.float8_e4m3fn).astype(np.float64)
    else:
        nib = np.empty((g, 128, n, 4), np.uint8)
        nib[..., 0::2] = words & 0xF
        nib[..., 1::2] = words >> 4
        vals = E2M1[nib]
    vals = vals * np.repeat(np.exp2(scales.astype(np.float64) - 127.0), 8, axis=1)[..., None]
    return vals.transpose(0, 1, 3, 2).reshape(g * 512, n)


K, R, N, T, J = 512, 512, 512, 1024, 512


def setup_inputs():
    n = np.random.standard_normal
    idx = np.random.permutation(T)[:J]
    fk = mx_kscale(K)
    fr = mx_kscale(R)
    fn = mx_kscale(N)
    xtp = pack_weight(n((K, T)) / fk[:, None], "e4m3")
    wap = pack_weight(n((K, R)) * 1 / np.sqrt(K) * fk[:, None] * fr, "e2m1")
    wdp = pack_weight(n((N, R)) * 1 / np.sqrt(N) * fn[:, None], "e4m3")
    wup = pack_weight(n((R, K)) * 1 / np.sqrt(R) / fr[:, None], "e2m1")
    return {
        "xt_words": xtp[0],
        "xt_scales": xtp[1],
        "wa_words": wap[0],
        "wa_scales": wap[1],
        "g": (n((N, T)) * np.exp(0.5 * n((1, T))) / fn[:, None]).astype(np.float32),
        "wd_words": wdp[0],
        "wd_scales": wdp[1],
        "wu_words": wup[0],
        "wu_scales": wup[1],
        "run": (0.3 * n((K, T))).astype(np.float32),
        "offs": striped(idx),
    }


def reference(xt_words, xt_scales, wa_words, wa_scales, g, wd_words, wd_scales, wu_words, wu_scales, run, offs):
    idx = unstriped(offs)
    xtu = unpack_weight(xt_words, xt_scales, "e4m3")
    wau = unpack_weight(wa_words, wa_scales, "e2m1")
    wdu = unpack_weight(wd_words, wd_scales, "e4m3")
    wuu = unpack_weight(wu_words, wu_scales, "e2m1")
    xtidxg = xtu[:, idx]
    a = wau.T @ xtidxg
    gidxq = mxq(f64(g)[:, idx], 0, "e5m2")
    d = wdu.T @ gidxq
    dz = 2.0 * d * np.maximum(a, 0.0)
    dzq = mxq(dz, 0, "e5m2")
    p = wuu.T @ dzq
    pp = np.zeros((K, T))
    pp[:, idx] = p
    y = pp + f64(run)
    return y

@@ -1,0 +1,230 @@
+from contextlib import ExitStack
+
+import concourse.mybir as mybir
+from concourse.masks import make_identity
+
+K, R, N, T, J = 512, 512, 512, 1024, 512
+FLOPS = 2 * J * (K * R + N * R + R * K)
+
+F32 = mybir.dt.float32
+BF16 = mybir.dt.bfloat16
+I32 = mybir.dt.int32
+U32 = mybir.dt.uint32
+U16 = mybir.dt.uint16
+U8 = mybir.dt.uint8
+E4M3 = mybir.dt.float8_e4m3fn_x4
+E5M2 = mybir.dt.float8_e5m2_x4
+E2M1 = mybir.dt.float4_e2m1fn_x4
+ACT = mybir.ActivationFunctionType
+ALU = mybir.AluOpType
+
+P = 128
+TILES = 4
+HALF = J // 2
+PIECE = T // 2
+LAST_SCALAR = 160
+WINDOWS = 3
+EARLY = 2
+
+
+def load_scale_rows(queue, plane, scales):
+    rows = scales[0].rearrange("(q r) c -> r q c", r=4)
+    for r in range(4):
+        queue.dma_start(out=plane[r:P:32, :].bitcast(I32), in_=rows[r].bitcast(I32))
+
+
+def tile_moe_expert_back_made_anew_kernel(
+    tc, xt_words, xt_scales, wa_words, wa_scales, g, wd_words, wd_scales, wu_words, wu_scales, run, offs, out
+):
+    nc = tc.nc
+    with ExitStack() as ctx:
+        keep = ctx.enter_context(tc.tile_pool(name="keep", bufs=1))
+        psum = ctx.enter_context(tc.psum_pool(name="psum", bufs=1))
+
+        offsets = keep.tile([P, J // 16], U16, name="offsets")
+        nc.sync.dma_start(offsets[:], offs)
+
+        x_scale = keep.tile([P, T], U8, name="x_scale", align_bytes=64)
+        wa_scale = keep.tile([P, R], U8, name="wa_scale", align_bytes=64)
+        wd_scale = keep.tile([P, R], U8, name="wd_scale", align_bytes=64)
+        wu_scale = keep.tile([P, K], U8, name="wu_scale", align_bytes=64)
+        for plane in (x_scale, wa_scale, wd_scale, wu_scale):
+            nc.gpsimd.memset(plane[:].bitcast(I32), 0)
+
+        x_word = keep.tile([P, T], U32, name="x_word", align_bytes=64)
+        nc.sync.dma_start(out=x_word[:].bitcast(I32), in_=xt_words[0].rearrange("p c t -> p (c t)").bitcast(I32))
+        load_scale_rows(nc.sync, x_scale, xt_scales)
+
+        wa_word = keep.tile([P, 2 * R], U8, name="wa_word", align_bytes=64)
+        g_rows = g.rearrange("(p f) t -> p f t", f=4)
+        g_raw = {}
+        for a in range(2):
+            for c in range(2):
+                if (a, c) == (1, 1):
+                    nc.sync.dma_start(out=wa_word[:].bitcast(I32), in_=wa_words[0].bitcast(I32))
+                    load_scale_rows(nc.sync, wa_scale, wa_scales)
+                g_raw[a, c] = keep.tile([P, 2, PIECE], F32, name="g_raw%d%d" % (a, c), tag="wide%d" % (2 * a + c))
+                nc.sync.dma_start(out=g_raw[a, c][:], in_=g_rows[:, 2 * a : 2 * a + 2, c * PIECE : (c + 1) * PIECE])
+
+        wd_word = keep.tile([P, R], U32, name="wd_word", align_bytes=64)
+        nc.sync.dma_start(out=wd_word[:].bitcast(I32), in_=wd_words[0].rearrange("p c t -> p (c t)").bitcast(I32))
+        load_scale_rows(nc.gpsimd, wd_scale, wd_scales)
+        wu_word = keep.tile([P, 2 * K], U8, name="wu_word", align_bytes=64)
+        nc.sync.dma_start(out=wu_word[:].bitcast(I32), in_=wu_words[0].bitcast(I32))
+        load_scale_rows(nc.sync, wu_scale, wu_scales)
+
+        identity = keep.tile([P, P], F32, name="identity")
+        make_identity(nc, identity[:])
+
+        windows = [keep.tile([P, T], F32, name="window%d" % kt) for kt in range(WINDOWS)]
+        for window in windows:
+            nc.vector.memset(window[:], 0.0)
+
+        banks = [psum.tile([P, 512], F32, name="bank%d" % b) for b in range(8)]
+
+        xg_word = keep.tile([P, J], U32, name="xg_word", align_bytes=64)
+        xg_scale = keep.tile([P, J], U8, name="xg_scale", align_bytes=64)
+        nc.vector.tensor_copy(xg_word[:], x_word[:].indirect(offsets[:]))
+        nc.vector.tensor_copy(xg_scale[:], x_scale[:].indirect(offsets[:]))
+
+        g_pair = [keep.tile([P, T], F32, name="g_pair%d" % a) for a in range(2)]
+        g_pick = [keep.tile([P, 2, HALF], F32, name="g_pick%d" % h) for h in range(2)]
+
+        def cast(engine_copy, a, c, lo, hi):
+            dst = g_pair[a][:].bitcast(BF16)[:, 2 * (c * PIECE + lo) : 2 * (c * PIECE + hi)]
+            engine_copy(dst.rearrange("p (c e) -> p c e", e=2), g_raw[a, c][:, :, lo:hi].rearrange("p e c -> p c e"))
+
+        def scalar_cast(dst, src):
+            nc.scalar.activation(out=dst, in_=src, func=ACT.Copy)
+
+        def vector_cast(dst, src):
+            nc.vector.tensor_copy(out=dst, in_=src)
+
+        for a in range(2):
+            cast(scalar_cast, a, 0, 0, PIECE)
+            if a == 0:
+                cast(scalar_cast, a, 1, 0, PIECE)
+            else:
+                cast(vector_cast, a, 1, 0, PIECE)
+            for h in range(2):
+                nc.vector.tensor_copy(g_pick[h][:, a, :], g_pair[a][:].indirect(offsets[:, 16 * h : 16 * (h + 1)]))
+
+        run_tiles = []
+        for kt in range(TILES):
+            run_tile = keep.tile([P, T], F32, name="run%d" % kt, tag="wide%d" % kt)
+            nc.sync.dma_start(out=run_tile[:], in_=run[kt * P : (kt + 1) * P, :])
+            run_tiles.append(run_tile)
+
+        relu2 = []
+        for jt in range(TILES):
+            cols = slice(jt * P, (jt + 1) * P)
+            nc.tensor.matmul_mx(
+                out=banks[jt][:],
+                lhsT=xg_word[:, cols].bitcast(E4M3),
+                lhsT_scale=xg_scale[:, cols],
+                rhs=wa_word[:].bitcast(E2M1),
+                rhs_scale=wa_scale[:],
+                start=True,
+                stop=True,
+            )
+            twice = keep.tile([P, R], F32, name="twice%d" % jt)
+            nc.scalar.activation(
+                out=twice[:].rearrange("j (u p e) -> j u p e", u=2, e=2),
+                in_=banks[jt][:].rearrange("j (p u e) -> j u p e", u=2, e=2),
+                func=ACT.Relu,
+                scale=2.0,
+            )
+            relu2.append(twice)
+
+        gq_word = keep.tile([P, J], U32, name="gq_word", align_bytes=64)
+        gq_scale = keep.tile([P, J], U8, name="gq_scale", align_bytes=64)
+        g_woven = [keep.tile([P, HALF, 2], F32, name="g_woven%d" % h, align_bytes=64) for h in range(2)]
+        for h in range(2):
+            nc.vector.tensor_copy(out=g_woven[h][:], in_=g_pick[h][:].rearrange("p a j -> p j a"))
+        for h in range(2):
+            cols = slice(h * HALF, (h + 1) * HALF)
+            nc.vector.quantize_mx(
+                out=gq_word[:, cols].bitcast(E5M2),
+                scales=gq_scale[:, cols],
+                in_=g_woven[h][:].rearrange("p j a -> p (j a)").bitcast(BF16),
+            )
+
+        dz_woven = [keep.tile([P, HALF * 2], F32, name="dz_woven%d" % h, align_bytes=64) for h in range(2)]
+        dzq_word = keep.tile([P, HALF + J], U32, name="dzq_word", align_bytes=64)
+        dzq_scale = keep.tile([P, HALF + J], U8, name="dzq_scale", align_bytes=64)
+        nc.gpsimd.memset(dzq_word[:, 0:HALF], 0)
+        nc.gpsimd.memset(dzq_scale[:, 0:HALF].bitcast(U32), 0)
+        for jt in range(TILES):
+            cols = slice(jt * P, (jt + 1) * P)
+            nc.tensor.matmul_mx(
+                out=banks[4 + jt][:],
+                lhsT=gq_word[:, cols].bitcast(E5M2),
+                lhsT_scale=gq_scale[:, cols],
+                rhs=wd_word[:].bitcast(E4M3),
+                rhs_scale=wd_scale[:],
+                start=True,
+                stop=True,
+            )
+
+        def way_back(kt, bank, first):
+            nc.tensor.matmul_mx(
+                out=bank[:],
+                lhsT=wu_word[:, 2 * P * kt : 2 * P * (kt + 1)].bitcast(E2M1),
+                lhsT_scale=wu_scale[:, kt * P : (kt + 1) * P],
+                rhs=dzq_word[:, first : first + J].bitcast(E5M2),
+                rhs_scale=dzq_scale[:, first : first + J],
+                start=True,
+                stop=True,
+            )
+
+        listed = [keep.tile([P, J], F32, name="listed%d" % kt) for kt in range(TILES)]
+        for jt in range(TILES):
+            dz_pair = keep.tile([P, R // 2], F32, name="dz_pair%d" % jt)
+            nc.vector.tensor_tensor(
+                out=dz_pair[:].bitcast(BF16).rearrange("j (u p e) -> j u p e", u=2, e=2),
+                in0=banks[4 + jt][:].rearrange("j (p u e) -> j u p e", u=2, e=2),
+                in1=relu2[jt][:].rearrange("j (u p e) -> j u p e", u=2, e=2),
+                op=ALU.mult,
+            )
+            for u in range(2):
+                nc.tensor.transpose(banks[jt][:, u * P : (u + 1) * P], dz_pair[:, u * P : (u + 1) * P], identity[:])
+            h, w = divmod(jt, 2)
+            nc.scalar.copy(
+                out=dz_woven[h][:, 2 * P * w : 2 * P * (w + 1)].rearrange("p (j u) -> p j u", u=2),
+                in_=banks[jt][:, 0 : 2 * P].rearrange("p (u j) -> p j u", u=2),
+            )
+            if w == 1:
+                cols = slice((h + 1) * HALF, (h + 2) * HALF)
+                nc.vector.quantize_mx(
+                    out=dzq_word[:, cols].bitcast(E5M2), scales=dzq_scale[:, cols], in_=dz_woven[h][:].bitcast(BF16)
+                )
+            if jt == 1:
+                for kt in range(EARLY):
+                    way_back(kt, banks[kt], 0)
+                    nc.scalar.copy(out=listed[kt][:, 0:HALF], in_=banks[kt][:, HALF:J])
+
+        for kt in range(TILES):
+            way_back(kt, banks[4 + kt], HALF)
+            first = HALF if kt < EARLY else 0
+            nc.scalar.copy(out=listed[kt][:, first:J], in_=banks[4 + kt][:, first:J])
+
+        for kt in range(EARLY):
+            nc.vector.tensor_copy(windows[kt][:].indirect(offsets[:, 0:16]), listed[kt][:, 0:HALF])
+        for kt in range(TILES):
+            window = windows[kt % WINDOWS]
+            if kt < EARLY:
+                nc.vector.tensor_copy(window[:].indirect(offsets[:, 16:32]), listed[kt][:, HALF:J])
+            else:
+                nc.vector.tensor_copy(window[:].indirect(offsets[:]), listed[kt][:])
+            total = keep.tile([P, T], F32, name="total%d" % kt)
+            rows = slice(kt * P, (kt + 1) * P)
+            if kt < TILES - 1:
+                nc.gpsimd.tensor_tensor(out=total[:], in0=window[:], in1=run_tiles[kt][:], op=ALU.add)
+                nc.sync.dma_start(out=out[rows, :], in_=total[:])
+            else:
+                for c in range(2):
+                    cols = slice(c * PIECE, (c + 1) * PIECE)
+                    nc.vector.tensor_tensor(
+                        out=total[:, cols], in0=window[:, cols], in1=run_tiles[kt][:, cols], op=ALU.add
+                    )
+                    nc.sync.dma_start(out=out[rows, cols], in_=total[:, cols])

@@ -210,6 +210,18 @@ def tile_moe_expert_back_made_anew_kernel(
 
         for kt in range(EARLY):
             nc.vector.tensor_copy(windows[kt][:].indirect(offsets[:, 0:16]), listed[kt][:, 0:HALF])
+
+        def turn(bank, source, c, start, stop, unit):
+            for b in range(4):
+                nc.tensor.matmul(
+                    bank[:, b * P : (b + 1) * P],
+                    lhsT=source[:, c * PIECE + b * P : c * PIECE + (b + 1) * P],
+                    rhs=unit[:],
+                    start=start and b == 0,
+                    stop=stop and b == 3,
+                    is_transpose=True,
+                )
+
         for kt in range(TILES):
             window = windows[kt % WINDOWS]
             if kt < EARLY:
@@ -219,8 +231,23 @@ def tile_moe_expert_back_made_anew_kernel(
             total = keep.tile([P, T], F32, name="total%d" % kt)
             rows = slice(kt * P, (kt + 1) * P)
             if kt < TILES - 1:
-                nc.gpsimd.tensor_tensor(out=total[:], in0=window[:], in1=run_tiles[kt][:], op=ALU.add)
-                nc.sync.dma_start(out=out[rows, :], in_=total[:])
+                sums = banks[2 * kt : 2 * kt + 2]
+                backs = banks[6:8]
+                turned = keep.tile([P, T], F32, name="turned%d" % kt, tag="turned%d" % kt)
+                held = identity
+                if kt == 2:
+                    held = keep.tile([P, P], F32, name="held", tag="turned1")
+                    nc.scalar.copy(out=held[:], in_=identity[:])
+                for c in range(2):
+                    turn(sums[c], run_tiles[kt], c, True, False, identity)
+                for c in range(2):
+                    turn(sums[c], window, c, False, True, held)
+                    nc.scalar.copy(out=turned[:, c * PIECE : (c + 1) * PIECE], in_=sums[c][:])
+                for c in range(2):
+                    cols = slice(c * PIECE, (c + 1) * PIECE)
+                    turn(backs[c], turned, c, True, True, identity)
+                    nc.scalar.copy(out=total[:, cols], in_=backs[c][:])
+                    nc.scalar.dma_start(out=out[rows, cols], in_=total[:, cols])
             else:
                 for c in range(2):
                     cols = slice(c * PIECE, (c + 1) * PIECE)

@@ -51,6 +51,10 @@ def tile_moe_expert_back_made_anew_kernel(
         for plane in (x_scale, wa_scale, wd_scale, wu_scale):
             nc.gpsimd.memset(plane[:].bitcast(I32), 0)
 
+        warm = keep.tile([P, 8], F32, name="warm")
+        nc.gpsimd.memset(warm[:], 0.0)
+        nc.scalar.activation(out=warm[:, 4:8], in_=warm[:, 0:4], func=ACT.Relu)
+
         x_word = keep.tile([P, T], U32, name="x_word", align_bytes=64)
         nc.sync.dma_start(out=x_word[:].bitcast(I32), in_=xt_words[0].rearrange("p c t -> p (c t)").bitcast(I32))
         load_scale_rows(nc.sync, x_scale, xt_scales)
@@ -68,7 +72,7 @@ def tile_moe_expert_back_made_anew_kernel(
 
         wd_word = keep.tile([P, R], U32, name="wd_word", align_bytes=64)
         nc.sync.dma_start(out=wd_word[:].bitcast(I32), in_=wd_words[0].rearrange("p c t -> p (c t)").bitcast(I32))
-        load_scale_rows(nc.gpsimd, wd_scale, wd_scales)
+        load_scale_rows(nc.sync, wd_scale, wd_scales)
         wu_word = keep.tile([P, 2 * K], U8, name="wu_word", align_bytes=64)
         nc.sync.dma_start(out=wu_word[:].bitcast(I32), in_=wu_words[0].bitcast(I32))
         load_scale_rows(nc.sync, wu_scale, wu_scales)
@@ -210,18 +214,6 @@ def tile_moe_expert_back_made_anew_kernel(
 
         for kt in range(EARLY):
             nc.vector.tensor_copy(windows[kt][:].indirect(offsets[:, 0:16]), listed[kt][:, 0:HALF])
-
-        def turn(bank, source, c, start, stop, unit):
-            for b in range(4):
-                nc.tensor.matmul(
-                    bank[:, b * P : (b + 1) * P],
-                    lhsT=source[:, c * PIECE + b * P : c * PIECE + (b + 1) * P],
-                    rhs=unit[:],
-                    start=start and b == 0,
-                    stop=stop and b == 3,
-                    is_transpose=True,
-                )
-
         for kt in range(TILES):
             window = windows[kt % WINDOWS]
             if kt < EARLY:
@@ -231,27 +223,12 @@ def tile_moe_expert_back_made_anew_kernel(
             total = keep.tile([P, T], F32, name="total%d" % kt)
             rows = slice(kt * P, (kt + 1) * P)
             if kt < TILES - 1:
-                sums = banks[2 * kt : 2 * kt + 2]
-                backs = banks[6:8]
-                turned = keep.tile([P, T], F32, name="turned%d" % kt, tag="turned%d" % kt)
-                held = identity
-                if kt == 2:
-                    held = keep.tile([P, P], F32, name="held", tag="turned1")
-                    nc.scalar.copy(out=held[:], in_=identity[:])
-                for c in range(2):
-                    turn(sums[c], run_tiles[kt], c, True, False, identity)
-                for c in range(2):
-                    turn(sums[c], window, c, False, True, held)
-                    nc.scalar.copy(out=turned[:, c * PIECE : (c + 1) * PIECE], in_=sums[c][:])
-                for c in range(2):
-                    cols = slice(c * PIECE, (c + 1) * PIECE)
-                    turn(backs[c], turned, c, True, True, identity)
-                    nc.scalar.copy(out=total[:, cols], in_=backs[c][:])
-                    nc.scalar.dma_start(out=out[rows, cols], in_=total[:, cols])
+                nc.gpsimd.tensor_tensor(out=total[:], in0=window[:], in1=run_tiles[kt][:], op=ALU.add)
+                nc.sync.dma_start(out=out[rows, :], in_=total[:])
             else:
                 for c in range(2):
                     cols = slice(c * PIECE, (c + 1) * PIECE)
                     nc.vector.tensor_tensor(
                         out=total[:, cols], in0=window[:, cols], in1=run_tiles[kt][:, cols], op=ALU.add
                     )
-                    nc.sync.dma_start(out=out[rows, cols], in_=total[:, cols])
+                    (nc.sync, nc.scalar)[c].dma_start(out=out[rows, cols], in_=total[:, cols])

from contextlib import ExitStack

import concourse.mybir as mybir
from concourse.masks import make_identity

K, R, N, T, J = 512, 512, 512, 1024, 512
FLOPS = 2 * J * (K * R + N * R + R * K)

F32 = mybir.dt.float32
BF16 = mybir.dt.bfloat16
I32 = mybir.dt.int32
U32 = mybir.dt.uint32
U16 = mybir.dt.uint16
U8 = mybir.dt.uint8
E4M3 = mybir.dt.float8_e4m3fn_x4
E5M2 = mybir.dt.float8_e5m2_x4
E2M1 = mybir.dt.float4_e2m1fn_x4
ACT = mybir.ActivationFunctionType
ALU = mybir.AluOpType

P = 128
TILES = 4
HALF = J // 2
PIECE = T // 2
LAST_SCALAR = 160
WINDOWS = 3
EARLY = 2


def load_scale_rows(queue, plane, scales):
    rows = scales[0].rearrange("(q r) c -> r q c", r=4)
    for r in range(4):
        queue.dma_start(out=plane[r:P:32, :].bitcast(I32), in_=rows[r].bitcast(I32))


def tile_moe_expert_back_made_anew_kernel(
    tc, xt_words, xt_scales, wa_words, wa_scales, g, wd_words, wd_scales, wu_words, wu_scales, run, offs, out
):
    nc = tc.nc
    with ExitStack() as ctx:
        keep = ctx.enter_context(tc.tile_pool(name="keep", bufs=1))
        psum = ctx.enter_context(tc.psum_pool(name="psum", bufs=1))

        offsets = keep.tile([P, J // 16], U16, name="offsets")
        nc.sync.dma_start(offsets[:], offs)

        x_scale = keep.tile([P, T], U8, name="x_scale", align_bytes=64)
        wa_scale = keep.tile([P, R], U8, name="wa_scale", align_bytes=64)
        wd_scale = keep.tile([P, R], U8, name="wd_scale", align_bytes=64)
        wu_scale = keep.tile([P, K], U8, name="wu_scale", align_bytes=64)
        for plane in (x_scale, wa_scale, wd_scale, wu_scale):
            nc.gpsimd.memset(plane[:].bitcast(I32), 0)

        warm = keep.tile([P, 8], F32, name="warm")
        nc.gpsimd.memset(warm[:], 0.0)
        nc.scalar.activation(out=warm[:, 4:8], in_=warm[:, 0:4], func=ACT.Relu)

        x_word = keep.tile([P, T], U32, name="x_word", align_bytes=64)
        nc.sync.dma_start(out=x_word[:].bitcast(I32), in_=xt_words[0].rearrange("p c t -> p (c t)").bitcast(I32))
        load_scale_rows(nc.sync, x_scale, xt_scales)

        wa_word = keep.tile([P, 2 * R], U8, name="wa_word", align_bytes=64)
        g_rows = g.rearrange("(p f) t -> p f t", f=4)
        g_raw = {}
        for a in range(2):
            for c in range(2):
                if (a, c) == (1, 1):
                    nc.sync.dma_start(out=wa_word[:].bitcast(I32), in_=wa_words[0].bitcast(I32))
                    load_scale_rows(nc.sync, wa_scale, wa_scales)
                g_raw[a, c] = keep.tile([P, 2, PIECE], F32, name="g_raw%d%d" % (a, c), tag="wide%d" % (2 * a + c))
                nc.sync.dma_start(out=g_raw[a, c][:], in_=g_rows[:, 2 * a : 2 * a + 2, c * PIECE : (c + 1) * PIECE])

        wd_word = keep.tile([P, R], U32, name="wd_word", align_bytes=64)
        nc.sync.dma_start(out=wd_word[:].bitcast(I32), in_=wd_words[0].rearrange("p c t -> p (c t)").bitcast(I32))
        load_scale_rows(nc.sync, wd_scale, wd_scales)
        wu_word = keep.tile([P, 2 * K], U8, name="wu_word", align_bytes=64)
        nc.sync.dma_start(out=wu_word[:].bitcast(I32), in_=wu_words[0].bitcast(I32))
        load_scale_rows(nc.sync, wu_scale, wu_scales)

        identity = keep.tile([P, P], F32, name="identity")
        make_identity(nc, identity[:])

        windows = [keep.tile([P, T], F32, name="window%d" % kt) for kt in range(WINDOWS)]
        for window in windows:
            nc.vector.memset(window[:], 0.0)

        banks = [psum.tile([P, 512], F32, name="bank%d" % b) for b in range(8)]

        xg_word = keep.tile([P, J], U32, name="xg_word", align_bytes=64)
        xg_scale = keep.tile([P, J], U8, name="xg_scale", align_bytes=64)
        nc.vector.tensor_copy(xg_word[:], x_word[:].indirect(offsets[:]))
        nc.vector.tensor_copy(xg_scale[:], x_scale[:].indirect(offsets[:]))

        g_pair = [keep.tile([P, T], F32, name="g_pair%d" % a) for a in range(2)]
        g_pick = [keep.tile([P, 2, HALF], F32, name="g_pick%d" % h) for h in range(2)]

        def cast(engine_copy, a, c, lo, hi):
            dst = g_pair[a][:].bitcast(BF16)[:, 2 * (c * PIECE + lo) : 2 * (c * PIECE + hi)]
            engine_copy(dst.rearrange("p (c e) -> p c e", e=2), g_raw[a, c][:, :, lo:hi].rearrange("p e c -> p c e"))

        def scalar_cast(dst, src):
            nc.scalar.activation(out=dst, in_=src, func=ACT.Copy)

        def vector_cast(dst, src):
            nc.vector.tensor_copy(out=dst, in_=src)

        for a in range(2):
            cast(scalar_cast, a, 0, 0, PIECE)
            if a == 0:
                cast(scalar_cast, a, 1, 0, PIECE)
            else:
                cast(vector_cast, a, 1, 0, PIECE)
            for h in range(2):
                nc.vector.tensor_copy(g_pick[h][:, a, :], g_pair[a][:].indirect(offsets[:, 16 * h : 16 * (h + 1)]))

        run_tiles = []
        for kt in range(TILES):
            run_tile = keep.tile([P, T], F32, name="run%d" % kt, tag="wide%d" % kt)
            nc.sync.dma_start(out=run_tile[:], in_=run[kt * P : (kt + 1) * P, :])
            run_tiles.append(run_tile)

        relu2 = []
        for jt in range(TILES):
            cols = slice(jt * P, (jt + 1) * P)
            nc.tensor.matmul_mx(
                out=banks[jt][:],
                lhsT=xg_word[:, cols].bitcast(E4M3),
                lhsT_scale=xg_scale[:, cols],
                rhs=wa_word[:].bitcast(E2M1),
                rhs_scale=wa_scale[:],
                start=True,
                stop=True,
            )
            twice = keep.tile([P, R], F32, name="twice%d" % jt)
            nc.scalar.activation(
                out=twice[:].rearrange("j (u p e) -> j u p e", u=2, e=2),
                in_=banks[jt][:].rearrange("j (p u e) -> j u p e", u=2, e=2),
                func=ACT.Relu,
                scale=2.0,
            )
            relu2.append(twice)

        gq_word = keep.tile([P, J], U32, name="gq_word", align_bytes=64)
        gq_scale = keep.tile([P, J], U8, name="gq_scale", align_bytes=64)
        g_woven = [keep.tile([P, HALF, 2], F32, name="g_woven%d" % h, align_bytes=64) for h in range(2)]
        for h in range(2):
            nc.vector.tensor_copy(out=g_woven[h][:], in_=g_pick[h][:].rearrange("p a j -> p j a"))
        for h in range(2):
            cols = slice(h * HALF, (h + 1) * HALF)
            nc.vector.quantize_mx(
                out=gq_word[:, cols].bitcast(E5M2),
                scales=gq_scale[:, cols],
                in_=g_woven[h][:].rearrange("p j a -> p (j a)").bitcast(BF16),
            )

        dz_woven = [keep.tile([P, HALF * 2], F32, name="dz_woven%d" % h, align_bytes=64) for h in range(2)]
        dzq_word = keep.tile([P, HALF + J], U32, name="dzq_word", align_bytes=64)
        dzq_scale = keep.tile([P, HALF + J], U8, name="dzq_scale", align_bytes=64)
        nc.gpsimd.memset(dzq_word[:, 0:HALF], 0)
        nc.gpsimd.memset(dzq_scale[:, 0:HALF].bitcast(U32), 0)
        for jt in range(TILES):
            cols = slice(jt * P, (jt + 1) * P)
            nc.tensor.matmul_mx(
                out=banks[4 + jt][:],
                lhsT=gq_word[:, cols].bitcast(E5M2),
                lhsT_scale=gq_scale[:, cols],
                rhs=wd_word[:].bitcast(E4M3),
                rhs_scale=wd_scale[:],
                start=True,
                stop=True,
            )

        def way_back(kt, bank, first):
            nc.tensor.matmul_mx(
                out=bank[:],
                lhsT=wu_word[:, 2 * P * kt : 2 * P * (kt + 1)].bitcast(E2M1),
                lhsT_scale=wu_scale[:, kt * P : (kt + 1) * P],
                rhs=dzq_word[:, first : first + J].bitcast(E5M2),
                rhs_scale=dzq_scale[:, first : first + J],
                start=True,
                stop=True,
            )

        listed = [keep.tile([P, J], F32, name="listed%d" % kt) for kt in range(TILES)]
        for jt in range(TILES):
            dz_pair = keep.tile([P, R // 2], F32, name="dz_pair%d" % jt)
            nc.vector.tensor_tensor(
                out=dz_pair[:].bitcast(BF16).rearrange("j (u p e) -> j u p e", u=2, e=2),
                in0=banks[4 + jt][:].rearrange("j (p u e) -> j u p e", u=2, e=2),
                in1=relu2[jt][:].rearrange("j (u p e) -> j u p e", u=2, e=2),
                op=ALU.mult,
            )
            for u in range(2):
                nc.tensor.transpose(banks[jt][:, u * P : (u + 1) * P], dz_pair[:, u * P : (u + 1) * P], identity[:])
            h, w = divmod(jt, 2)
            nc.scalar.copy(
                out=dz_woven[h][:, 2 * P * w : 2 * P * (w + 1)].rearrange("p (j u) -> p j u", u=2),
                in_=banks[jt][:, 0 : 2 * P].rearrange("p (u j) -> p j u", u=2),
            )
            if w == 1:
                cols = slice((h + 1) * HALF, (h + 2) * HALF)
                nc.vector.quantize_mx(
                    out=dzq_word[:, cols].bitcast(E5M2), scales=dzq_scale[:, cols], in_=dz_woven[h][:].bitcast(BF16)
                )
            if jt == 1:
                for kt in range(EARLY):
                    way_back(kt, banks[kt], 0)
                    nc.scalar.copy(out=listed[kt][:, 0:HALF], in_=banks[kt][:, HALF:J])

        for kt in range(TILES):
            way_back(kt, banks[4 + kt], HALF)
            first = HALF if kt < EARLY else 0
            nc.scalar.copy(out=listed[kt][:, first:J], in_=banks[4 + kt][:, first:J])

        for kt in range(EARLY):
            nc.vector.tensor_copy(windows[kt][:].indirect(offsets[:, 0:16]), listed[kt][:, 0:HALF])
        for kt in range(TILES):
            window = windows[kt % WINDOWS]
            if kt < EARLY:
                nc.vector.tensor_copy(window[:].indirect(offsets[:, 16:32]), listed[kt][:, HALF:J])
            else:
                nc.vector.tensor_copy(window[:].indirect(offsets[:]), listed[kt][:])
            total = keep.tile([P, T], F32, name="total%d" % kt)
            rows = slice(kt * P, (kt + 1) * P)
            if kt < TILES - 1:
                nc.gpsimd.tensor_tensor(out=total[:], in0=window[:], in1=run_tiles[kt][:], op=ALU.add)
                nc.sync.dma_start(out=out[rows, :], in_=total[:])
            else:
                for c in range(2):
                    cols = slice(c * PIECE, (c + 1) * PIECE)
                    nc.vector.tensor_tensor(
                        out=total[:, cols], in0=window[:, cols], in1=run_tiles[kt][:, cols], op=ALU.add
                    )
                    (nc.sync, nc.scalar)[c].dma_start(out=out[rows, cols], in_=total[:, cols])
